import numpy as np, ml_dtypes
CORES = [12,28,44,60,3,19,35,51]
N = 8
TK, LAY = 128, 3
def setup_inputs(rng):
    return {"x": rng.standard_normal((N, 128, TK), dtype=np.float32).astype(ml_dtypes.bfloat16), "w": (rng.standard_normal((N, 128, LAY * 256), dtype=np.float32) / 16).astype(ml_dtypes.bfloat16)}
def setup_inputs_big(rng):
    d = setup_inputs(rng)
    for k in ("x",): d[k] = (d[k].astype(np.float32) * 1048576.0).astype(d[k].dtype)
    return d
def setup_inputs_small(rng):
    d = setup_inputs(rng)
    for k in ("x",): d[k] = (d[k].astype(np.float32) * (1 / 1048576.0)).astype(d[k].dtype)
    return d
def setup_inputs_apart(rng):
    d = setup_inputs(rng)
    f = (10.0 ** rng.permutation(np.linspace(-1.5, 1.5, N))).astype(np.float32).reshape(N, 1, 1)
    for k in ("x",): d[k] = (d[k].astype(np.float32) * f).astype(d[k].dtype)
    return d
def reference(x, w):
    X, W = x.astype(np.float64), w.astype(np.float64)
    h = list(X)
    for l in range(LAY):
        h = [np.maximum(W[r][:, 256 * l:256 * l + 128].T @ h[r] + W[r][:, 256 * l + 128:256 * l + 256].T @ h[r ^ (1 << l)], 0.0) for r in range(N)]
    return {"y": np.stack(h).astype(ml_dtypes.bfloat16)}

from concourse.bass import DstId, RemoteDMATransfer
from concourse.mybir import AluOpType

SIM_CORES = 64
TK = 128
BF, F32 = "bfloat16", "float32"

SCRATCH = {
    "xs": ("sbuf", [128, TK], BF),
    "ws": ("sbuf", [128, 768], BF),
    "zero": ("sbuf", [128, TK], F32),
    "in0": ("sbuf", [128, TK], BF),
    "in1": ("sbuf", [128, TK], BF),
    "in2": ("sbuf", [128, TK], BF),
    "h1": ("sbuf", [128, TK], BF),
    "h2": ("sbuf", [128, TK], BF),
    "h3": ("sbuf", [128, TK], BF),
    "wpu": ("sbuf", [128, TK], BF),
    "wpv": ("sbuf", [128, TK], BF),
    "ha": ("sbuf", [128, TK], BF),
    "hb": ("sbuf", [128, TK], BF),
    "h2p": ("sbuf", [128, TK], BF),
    "rw": ("sbuf", [128, TK], BF),
    "rh": ("sbuf", [128, TK], BF),
    "p0": ("psum", [128, 512], F32),
    "p1": ("psum", [128, 512], F32),
    "p2": ("psum", [128, 512], F32),
    "p3": ("psum", [128, 512], F32),
}
SEMAPHORES = ["sx", "sw01", "sw2", "sy", "sz", "left",
              "a0", "a1", "a2", "awu", "awv", "aha", "ahb", "rwa", "rha",
              "m0", "m1", "m2", "m3", "v0", "v1", "v2", "v3"]


def _engines(mask):
    return [1 << i for i in range(mask.bit_length()) if (mask >> i) & 1]


def rank_program(g, core, T, topo):
    cores = list(T.cores)
    S = T.sem
    sent = [0]

    def blocked(r):
        return not topo.may_write(cores[r], cores[r ^ 4])

    def ports(r):
        c = cores[r]
        ok = [k for k in range(SIM_CORES)
              if k not in cores and topo.chip(k) == topo.chip(c) and topo.die(k) == topo.die(c)
              and topo.may_write(k, cores[r ^ 4]) and topo.may_write(k, cores[r ^ 6])]
        return ok[0], ok[1]

    def send(dst, out, in_, sem):
        rid, pid, _ = topo.addr(dst)
        m = topo.mask(core, dst)
        n = len(_engines(m))
        g.remote_dma(out_ap=out, in_ap=in_, remote_sem=sem, local_sem=S.left, pid=pid, routing_id=rid,
                     dma_engine_mask=m)
        sent[0] += n
        return n

    def send_pair(dsts, outs, ins, sem):
        trs = []
        for i, d in enumerate(dsts):
            rid, pid, _ = topo.addr(d)
            e = _engines(topo.mask(core, d))
            half = len(e) // 2
            m = sum(e[i * half:(i + 1) * half])
            trs.append(RemoteDMATransfer(dst_ids=[DstId(rid=rid, pnc=pid)], dma_engine_mask=m, remote_sem=sem,
                                         src=ins[i], dst=outs[i]))
            sent[0] += half
        g.remote_dma_fused(trs, local_sem=S.left)

    def arrives(src, dst, parts=1):
        return len(_engines(topo.mask(src, dst))) // parts

    rank = T.rank_of(core)

    if rank is None:
        for r in range(len(cores)):
            if not blocked(r):
                continue
            pa, pb = ports(r)
            if core not in (pa, pb):
                continue
            first = core == pa
            g.wait_ge(S.rwa, arrives(cores[r], core, 2))
            send(cores[r ^ 4], (T.wpu if first else T.wpv)[:], T.rw[:], S.awu if first else S.awv)
            g.wait_ge(S.rha, arrives(cores[r], core, 2))
            if first:
                send(cores[r ^ 4], T.ha[:], T.rh[:], S.aha)
            else:
                send(cores[r ^ 6], T.hb[:], T.rh[:], S.ahb)
            g.wait_ge(S.left, sent[0])
        return

    r = rank
    mine_blocked = blocked(r)
    peer_blocked = blocked(r ^ 4)
    te, ve, sy = g.tensor, g.vector, g.sync

    def u(l):
        return T.ws[:, 256 * l:256 * l + 128]

    def v(l):
        return T.ws[:, 256 * l + 128:256 * l + 256]

    def relu(out, acc, after, done):
        ve.wait_ge(after, 1)
        ve.tensor_tensor(out[:], acc[:, 0:TK], T.zero[:], AluOpType.max).then_inc(done, 1)

    sy.dma_start(T.xs[:], T.x[:]).then_inc(S.sx, 16)
    sy.dma_start(T.ws[:, 0:512], T.w[:, 0:512]).then_inc(S.sw01, 16)
    sy.dma_start(T.ws[:, 512:768], T.w[:, 512:768]).then_inc(S.sw2, 16)
    ve.memset(T.zero[:], 0.0).then_inc(S.sz, 1)
    ve.wait_ge(S.sz, 1)

    g.wait_ge(S.sx, 16)
    send(cores[r ^ 1], T.in0[:], T.xs[:], S.a0)
    if mine_blocked:
        pa, pb = ports(r)
        g.wait_ge(S.sw01, 16)
        send_pair((pa, pb), (T.rw[:], T.rw[:]), (u(1), v(1)), S.rwa)
    te.wait_ge(S.sx, 16)
    te.wait_ge(S.sw01, 16)
    te.matmul(T.p0[:, 0:TK], u(0), T.xs[:], True, False)
    te.wait_ge(S.a0, arrives(cores[r ^ 1], core))
    te.matmul(T.p0[:, 0:TK], v(0), T.in0[:], False, True).then_inc(S.m0, 1)
    relu(T.h1, T.p0, S.m0, S.v0)

    g.wait_ge(S.v0, 1)
    if mine_blocked:
        send_pair((pa, pb), (T.rh[:], T.rh[:]), (T.h1[:], T.h1[:]), S.rha)
    send(cores[r ^ 2], T.in1[:], T.h1[:], S.a1)
    te.wait_ge(S.v0, 1)
    te.matmul(T.p1[:, 0:TK], u(1), T.h1[:], True, False)
    te.wait_ge(S.a1, arrives(cores[r ^ 2], core))
    te.matmul(T.p1[:, 0:TK], v(1), T.in1[:], False, True).then_inc(S.m1, 1)
    relu(T.h2, T.p1, S.m1, S.v1)

    if not mine_blocked:
        g.wait_ge(S.v1, 1)
        send(cores[r ^ 4], T.in2[:], T.h2[:], S.a2)
    te.wait_ge(S.v1, 1)
    te.wait_ge(S.sw2, 16)
    te.matmul(T.p2[:, 0:TK], u(2), T.h2[:], True, False)
    if peer_blocked:
        qa, _ = ports(r ^ 4)
        _, qb4 = ports(r ^ 4)
        _, qb6 = ports(r ^ 6)
        te.wait_ge(S.awu, arrives(qa, core))
        te.wait_ge(S.aha, arrives(qa, core))
        te.matmul(T.p3[:, 0:TK], T.wpu[:], T.ha[:], True, False)
        te.wait_ge(S.awv, arrives(qb4, core))
        te.wait_ge(S.ahb, arrives(qb6, core))
        te.matmul(T.p3[:, 0:TK], T.wpv[:], T.hb[:], False, True).then_inc(S.m3, 1)
        relu(T.h2p, T.p3, S.m3, S.v3)
        te.wait_ge(S.v3, 1)
        other = T.h2p
    else:
        te.wait_ge(S.a2, arrives(cores[r ^ 4], core))
        other = T.in2
    te.matmul(T.p2[:, 0:TK], v(2), other[:], False, True).then_inc(S.m2, 1)
    relu(T.h3, T.p2, S.m2, S.v2)

    sy.wait_ge(S.v2, 1)
    sy.dma_start(T.y[:], T.h3[:]).then_inc(S.sy, 16)
    sy.wait_ge(S.sy, 16)
    g.wait_ge(S.left, sent[0])
